import numpy as np
import ml_dtypes


def mxq(x, axis, fmt="e4m3"):
    dtype, down = {"e4m3": (ml_dtypes.float8_e4m3fn, 7), "e5m2": (ml_dtypes.float8_e5m2, 14)}[fmt]
    v = np.moveaxis(np.asarray(x, np.float32).astype(ml_dtypes.bfloat16).astype(np.float64), axis, -1)
    blocks = v.reshape(v.shape[:-1] + (-1, 32))
    amax = np.abs(blocks).max(-1, keepdims=True)
    byte = np.maximum(np.where(amax > 0, np.frexp(amax)[1] - 1 + 127, 0) - down, 1)
    scale = np.exp2(byte - 127.0)
    codes = (blocks / scale).astype(np.float32).astype(dtype).astype(np.float64)
    return np.moveaxis((codes * scale).reshape(v.shape), -1, axis)


WIDE = False


def mx_kscale(k):
    if not WIDE:
        return np.ones(k)
    levels = np.array([10, -10, 5, -5, 0])
    if k % 512:
        return np.exp2(np.random.permutation(np.resize(levels, k // 32))).repeat(32)
    a = np.empty((k // 512, 16))
    for p in range(k // 512):
        a[p, :8] = np.random.permutation(np.resize(levels, 8))
        for g in range(8):
            far = levels[np.abs(levels - a[p, g]) >= 10]
            a[p, g + 8] = far[np.random.randint(len(far))]
    return np.exp2(a.ravel()).repeat(32)


def f64(x):
    return np.asarray(x).astype(np.float64)


def striped(idx):
    return np.tile(idx.reshape(-1, 16).T, (8, 1)).astype(np.uint16)


def unstriped(offs):
    return offs[:16].T.reshape(-1).astype(np.int64)


def pack_weight(w):
    k, n = w.shape
    w = f64(np.asarray(w, np.float32).astype(ml_dtypes.bfloat16)).reshape(k // 32, 32, n)
    amax = np.abs(w).max(1)
    byte = np.clip(np.where(amax > 0, np.frexp(amax)[1] - 1 + 127 - 7, 1), 1, 254)
    scaled = (w * np.exp2(127.0 - byte)[:, None, :]).reshape(k, n).astype(np.float32)
    words = np.ascontiguousarray(scaled.reshape(k // 512, 128, 4, n).transpose(0, 1, 3, 2)).astype(ml_dtypes.float8_e4m3fn).view(np.uint8)
    return words, np.ascontiguousarray(byte.astype(np.uint8).reshape(k // 512, 16, n))


def unpack_weight(words, scales):
    g, p, n, _ = words.shape
    vals = np.ascontiguousarray(words).view(ml_dtypes.float8_e4m3fn).astype(np.float64) * np.repeat(np.exp2(scales.astype(np.float64) - 127.0), 8, axis=1)[..., None]
    return vals.transpose(0, 1, 3, 2).reshape(g * 512, n)


K, T, S, V, H, W = 512, 2048, 512, 256, 512, 192


def setup_inputs():
    n = np.random.standard_normal
    s = mx_kscale(K)[:, None]
    u = mx_kscale(S)
    packed_xT = pack_weight(n((K, T)) * s)
    return {
        "x_words": packed_xT[0],
        "x_scales": packed_xT[1],
        "w1": (n((K, H)) / np.sqrt(K) / s).astype(np.float32),
        "w2": (n((K, H)) / np.sqrt(K) / s).astype(np.float32),
        "w3": (n((K, H)) / np.sqrt(K) / s).astype(np.float32),
        "ga": (np.random.uniform(0.5, 1.5, (H, 1)) * u[:, None]).astype(np.float32),
        "gb": (np.random.uniform(0.5, 1.5, (H, 1)) / u[:, None]).astype(np.float32),
        "offs": striped(np.random.permutation(T)[:S]),
        "two": striped(np.random.permutation(T)[:S]),
        "n1": striped(np.random.permutation(S)),
        "n2": striped(np.random.permutation(S)),
        "three": striped(np.random.permutation(T)[:V]),
        "n3": striped(np.random.permutation(V)[:W]),
        "n4": striped(np.random.permutation(V)[:W]),
        "n5": striped(np.random.permutation(V)),
        "n6": striped(np.random.permutation(V)),
        "n7": striped(np.random.permutation(V)),
    }


def reference(x_words, x_scales, w1, w2, w3, ga, gb, offs, two, n1, n2, three, n3, n4, n5, n6, n7):
    xq = unpack_weight(x_words, x_scales)[:, unstriped(offs)]
    y = mxq(f64(w1), 0, "e4m3").T @ xq
    x_two = unpack_weight(x_words, x_scales)[:, unstriped(two)]
    d = mxq(f64(w2), 0, "e4m3").T @ x_two
    z = f64(ga) * ((y - y[:, unstriped(n1)]) / (np.abs(d) + np.abs(d[:, unstriped(n2)]) + 0.5))
    x_three = unpack_weight(x_words, x_scales)[:, unstriped(three)]
    b = mxq(f64(w3), 0, "e4m3").T @ x_three
    pa = b[:, unstriped(n4)]
    old = b[:, unstriped(n3)]
    ra = np.minimum(pa, old) - (0.5 * pa)
    ds = b.copy()
    ds[:, unstriped(n3)] = ra
    z2 = f64(gb) * ds
    s = 0.0625 * ((mxq(z, 0, "e4m3").T @ mxq(z2, 0, "e4m3")))
    st = s - s[:, unstriped(n5)]
    su = np.maximum(st, st[:, unstriped(n6)])
    return su + 0.5 * su[:, unstriped(n7)]

@@ -1,0 +1,349 @@
+from contextlib import ExitStack
+
+import concourse.mybir as mybir
+from concourse.masks import make_identity
+
+K, T, S, V, H, W = 512, 2048, 512, 256, 512, 192
+FLOPS = 2 * K * H * (2 * S + V) + 2 * H * S * V
+
+F32 = mybir.dt.float32
+BF16 = mybir.dt.bfloat16
+I32 = mybir.dt.int32
+U32 = mybir.dt.uint32
+U16 = mybir.dt.uint16
+U8 = mybir.dt.uint8
+FP8X4 = mybir.dt.float8_e4m3fn_x4
+ACT = mybir.ActivationFunctionType
+ALU = mybir.AluOpType
+
+P = 128
+PACK = 4
+TILES = H // P
+HALF = 256
+
+
+def tile_picked_twknormbkminthree_none_p_kernel(
+    tc, x_words, x_scales, w1, w2, w3, ga, gb, offs, two, n1, n2, three, n3, n4, n5, n6, n7, out
+):
+    nc = tc.nc
+    with ExitStack() as ctx:
+        keep = ctx.enter_context(tc.tile_pool(name="keep", bufs=1))
+        psum = ctx.enter_context(tc.psum_pool(name="psum", bufs=1))
+
+        def sb(name, shape, dtype, tag=None):
+            return keep.tile(shape, dtype, name=name, tag=tag or name, align_bytes=64)
+
+        def bank(name, number):
+            return psum.tile([P, 512], F32, name=name, tag=f"bank{number}")
+
+        def load_list(name, src):
+            t = sb(name, list(src.shape), U16)
+            nc.sync.dma_start(t[:], src)
+            return t
+
+        def load_weight_half(name, w, h):
+            raw = sb(name, [P, PACK, HALF], F32)
+            nc.sync.dma_start(raw[:], w[:, HALF * h : HALF * (h + 1)].rearrange("(p j) c -> p j c", j=PACK))
+            return raw
+
+        xs = sb("xs", [P, T], U8)
+        nc.gpsimd.memset(xs[:].bitcast(I32), 0)
+        w1_raw, w2_raw, w3_raw = [], [], []
+        l_two = load_list("l_two", two)
+        xw = sb("xw", [P, T], U32)
+        nc.sync.dma_start(xw[:].bitcast(I32), x_words[0].rearrange("p n t -> p (n t)").bitcast(I32))
+        for q in range(4):
+            nc.scalar.dma_start(xs[32 * q : 32 * q + 4, :].bitcast(I32), x_scales[0, 4 * q : 4 * q + 4, :].bitcast(I32))
+        ga_sb = sb("ga_sb", [P, TILES], F32)
+        with nc.allow_non_contiguous_dma(reason="one value a partition"):
+            nc.gpsimd.dma_start(ga_sb[:], ga.rearrange("(t p) o -> p (t o)", p=P))
+        gb_sb = sb("gb_sb", [P, TILES], F32)
+        nc.gpsimd.dma_start(gb_sb[:], gb.rearrange("(p t) o -> p (t o)", t=TILES))
+        w2_raw.append(load_weight_half("w2_raw0", w2, 0))
+        w2_raw.append(load_weight_half("w2_raw1", w2, 1))
+        l_offs = load_list("l_offs", offs)
+        w1_raw.append(load_weight_half("w1_raw0", w1, 0))
+        w1_raw.append(load_weight_half("w1_raw1", w1, 1))
+        l_three = load_list("l_three", three)
+        w3_raw.append(load_weight_half("w3_raw0", w3, 0))
+        w3_raw.append(load_weight_half("w3_raw1", w3, 1))
+        l_n1 = load_list("l_n1", n1)
+        l_n4 = load_list("l_n4", n4)
+        l_n3 = load_list("l_n3", n3)
+        l_n2 = load_list("l_n2", n2)
+        l_n5 = load_list("l_n5", n5)
+        l_n6 = load_list("l_n6", n6)
+        l_n7 = load_list("l_n7", n7)
+        ident = sb("ident", [P, P], F32)
+        make_identity(nc, ident[:])
+
+        scalar_copy, vector_copy = nc.scalar.copy, nc.vector.tensor_copy
+
+        def pick_words(name, lst, n, tag=None):
+            words = sb(name + "_words", [P, n], U32, tag)
+            nc.vector.tensor_copy(words[:], xw[:].indirect(lst[:]))
+            return words
+
+        def pick_scales(name, lst, n, tag=None):
+            scales = sb(name + "_scales", [P, n], U8, tag)
+            nc.vector.tensor_copy(scales[:], xs[:].indirect(lst[:]))
+            return scales
+
+        def pick(name, lst, n):
+            return pick_words(name, lst, n), pick_scales(name, lst, n)
+
+        def quantize(name, grouped, n):
+            codes = sb(name + "_codes", [P, n], U32)
+            scales = sb(name + "_sc", [P, n], U8)
+            nc.vector.quantize_mx(out=codes[:].bitcast(FP8X4), scales=scales[:], in_=grouped)
+            return codes, scales
+
+        def cast_plain(name, raw, copy):
+            grouped = sb(name, [P, HALF * PACK], BF16)
+            copy(
+                grouped[:].rearrange("p (c i j) -> p c j i", i=4, j=PACK),
+                raw[:].rearrange("p j (c i) -> p c j i", i=4),
+            )
+            return grouped
+
+        def cast_dealt(h, copy):
+            copy(
+                w3_grouped[:, :, 64 * h : 64 * (h + 1), :].rearrange("p t m j -> p m j t"),
+                w3_raw[h][:].rearrange("p j (m t) -> p m j t", t=TILES),
+            )
+
+        def mm(dst, lhs, m0, rhs, n):
+            nc.tensor.matmul_mx(
+                out=dst,
+                lhsT=lhs[0][:, m0 : m0 + P].bitcast(FP8X4),
+                lhsT_scale=lhs[1][:, m0 : m0 + P],
+                rhs=rhs[0][:, 0:n].bitcast(FP8X4),
+                rhs_scale=rhs[1][:, 0:n],
+                start=True,
+                stop=True,
+            )
+
+        def gather_s(dst, window, lst, scale=1.0):
+            nc.scalar.activation(dst, window[:].indirect(lst), ACT.Copy, scale=scale)
+
+        def gather_v(dst, window, lst):
+            nc.vector.tensor_copy(dst, window[:].indirect(lst))
+
+        w3_grouped = sb("w3_grouped", [P, TILES, P, PACK], BF16)
+        b = [sb(f"b{t}", [P, V], F32) for t in range(TILES)]
+        pa = [sb(f"pa{pair}", [P, 2 * W], F32) for pair in range(2)]
+        old = [sb(f"old{pair}", [P, 2 * W], F32) for pair in range(2)]
+        late = [sb(f"late{pair}", [P, 2 * HALF], F32) for pair in range(2)]
+        ra = [late[pair][:, 0 : 2 * W] for pair in range(2)]
+        size = [sb(f"size{t}", [P, S], F32) for t in range(TILES)]
+        size_at = [
+            [sb(f"size_at{t}", [P, HALF], F32)[:] for t in range(TILES)],
+            [(pa, old)[t % 2][t // 2][:, 0:HALF] for t in range(TILES)],
+        ]
+        y = [sb(f"y{t}", [P, S], F32) for t in range(TILES)]
+        y_at = [
+            [sb(f"y_at{t}", [P, HALF], F32)[:] for t in range(TILES)],
+            [sb(f"y_late{t}", [P, HALF], F32)[:] for t in range(2)] + [late[1][:, HALF * e : HALF * (e + 1)] for e in range(2)],
+        ]
+        once_late = sb("once_late", [P, 2 * H], F32)
+        z2_grouped = once_late[:, HALF : HALF + H].bitcast(BF16)
+        staged = sb("staged", [P, TILES * V], BF16)
+        z2_rows = staged[:].rearrange("p (t v) -> p t v", t=TILES)
+
+        def d_tile(t, wq, xq):
+            acc = bank(f"d_acc{t}", t)
+            mm(acc[:], wq, P * (t % 2), xq, S)
+            nc.scalar.activation(size[t][:], acc[:], ACT.Abs)
+
+        def y_tile(t, wq, xq, on_scalar):
+            acc = bank(f"y_acc{t}", 4 + t)
+            mm(acc[:], wq, P * (t % 2), xq, S)
+            if on_scalar:
+                nc.scalar.activation(y[t][:], acc[:], ACT.Copy, scale=ga_sb[:, t : t + 1])
+            else:
+                nc.vector.tensor_scalar(y[t][:], acc[:], ga_sb[:, t : t + 1], None, ALU.mult)
+
+        def b_pair(pair, wq, xq, copy):
+            acc = bank(f"b_acc{pair}", pair)
+            for e in range(2):
+                mm(acc[:, V * e : V * (e + 1)], wq, P * (2 * pair + e), xq, V)
+            for e in range(2):
+                copy(b[2 * pair + e][:], acc[:, V * e : V * (e + 1)])
+
+        def b_look(pair):
+            for e in range(2):
+                gather_s(pa[pair][:, W * e : W * (e + 1)], b[2 * pair + e], l_n4[:])
+                gather_s(old[pair][:, W * e : W * (e + 1)], b[2 * pair + e], l_n3[:])
+
+        least = [sb(f"least{pair}", [P, 2 * W], F32) for pair in range(2)]
+
+        def least_pair(pair):
+            nc.vector.tensor_tensor(least[pair][:], pa[pair][:], old[pair][:], ALU.min)
+
+        def ra_pair(pair):
+            nc.vector.scalar_tensor_tensor(ra[pair], pa[pair][:], -0.5, least[pair][:], ALU.mult, ALU.add)
+
+        def put(t):
+            nc.scalar.activation(b[t][:].indirect(l_n3[:]), ra[t // 2][:, W * (t % 2) : W * (t % 2 + 1)], ACT.Copy)
+
+        def z2_tile(t):
+            nc.vector.tensor_scalar(z2_rows[:, t, :], b[t][:], gb_sb[:, t : t + 1], None, ALU.mult)
+
+        def z2_quantize():
+            nc.vector.tensor_copy(
+                z2_grouped.rearrange("p (c i t) -> p c t i", i=4, t=PACK),
+                z2_rows.rearrange("p t (c i) -> p c t i", i=4),
+            )
+            return quantize("z2q", z2_grouped, V)
+
+        def size_look(t, h):
+            gather_v(size_at[h][t], size[t], l_n2[:, 16 * h : 16 * (h + 1)])
+
+        def y_look(t, h):
+            gather_s(y_at[h][t], y[t], l_n1[:, 16 * h : 16 * (h + 1)], scale=-1.0)
+
+        def add_transposed(dst, first, second, i):
+            cols = slice(P * i, P * (i + 1))
+            in_half = slice(P * (i % 2), P * (i % 2 + 1))
+            for t in range(TILES):
+                o = dst[:, P * t : P * (t + 1)]
+                nc.tensor.matmul(o, first[t][:, in_half], ident[:], start=True, stop=False, is_transpose=True)
+                nc.tensor.matmul(o, second[t][:, cols], ident[:], start=False, stop=True, is_transpose=True)
+
+        DEALT = "p (u m e) -> p u m e"
+        PLAIN = "p (m u e) -> p u m e"
+
+        def root_block(i):
+            total = bank(f"total{i}", 2 + i % 2)
+            add_transposed(total, size_at[i // 2], size, i)
+            root = sb(f"root{i}", [P, H], F32)
+            nc.scalar.activation(
+                root[:].rearrange(DEALT, u=2, e=2), total[:].rearrange(PLAIN, u=2, e=2), ACT.Abs_reciprocal_sqrt, bias=0.5
+            )
+            return root
+
+        def once_block(i, root):
+            diff = bank(f"diff{i}", 4 + i)
+            add_transposed(diff, y_at[i // 2], y, i)
+            once = once_late[:, H * (i - 2) : H * (i - 1)] if i >= 2 else sb(f"once{i}", [P, H], F32)[:]
+            nc.vector.tensor_tensor(
+                once.rearrange(DEALT, u=2, e=2),
+                diff[:].rearrange(PLAIN, u=2, e=2),
+                root[:].rearrange(DEALT, u=2, e=2),
+                ALU.mult,
+            )
+            return once
+
+        def z_block(i, once, root):
+            z_rows = sb(f"z_rows{i}", [P, H], BF16)
+            nc.vector.tensor_tensor(z_rows[:], once, root[:], ALU.mult)
+            return z_rows
+
+        def zg_block(i, z_rows, copy):
+            turned = bank(f"turned{i}", 4 + (i + 2) % 4)
+            words = z_rows[:].bitcast(F32)
+            for u in range(2):
+                nc.tensor.transpose(turned[:, P * u : P * (u + 1)], words[:, P * u : P * (u + 1)], ident[:])
+            z_grouped = staged[:, H * i : H * (i + 1)] if i < 2 else sb(f"z_grouped{i}", [P, H], BF16)[:]
+            copy(
+                z_grouped.bitcast(F32).rearrange("p (r u) -> p r u", u=2),
+                turned[:, 0 : 2 * P].rearrange("p (u r) -> p r u", u=2),
+            )
+            return z_grouped
+
+        def zq_block(i, z_grouped):
+            return quantize(f"zq{i}", z_grouped, P)
+
+        def s_block(i, zq, on_scalar):
+            acc = bank(f"s_acc{i}", i)
+            mm(acc[:, 0:V], zq, 0, z2q, V)
+            if on_scalar:
+                nc.scalar.activation(s[i][:], acc[:, 0:V], ACT.Copy, scale=0.0625)
+            else:
+                nc.vector.tensor_scalar(s[i][:], acc[:, 0:V], 0.0625, None, ALU.mult)
+
+        s, s_at, st, st_at, su, su_at, res = [
+            [sb(f"{name}{i}", [P, V], F32) for i in range(4)] for name in ("s", "s_at", "st", "st_at", "su", "su_at", "res")
+        ]
+        parts = [(slice(P * h, P * (h + 1)), slice(8 * h, 8 * (h + 1))) for h in range(2)]
+
+        def s_look(i):
+            for cols, entries in parts:
+                gather_s(s_at[i][:, cols], s[i], l_n5[:, entries])
+
+        def st_block(i):
+            nc.vector.tensor_tensor(st[i][:], s[i][:], s_at[i][:], ALU.subtract)
+
+        def st_look(i, gather):
+            for cols, entries in parts:
+                gather(st_at[i][:, cols], st[i], l_n6[:, entries])
+
+        def su_block(i):
+            nc.vector.tensor_tensor(su[i][:], st[i][:], st_at[i][:], ALU.max)
+
+        def su_look(i):
+            for cols, entries in parts:
+                gather_s(su_at[i][:, cols], su[i], l_n7[:, entries], scale=0.5)
+
+        def out_block(i):
+            nc.vector.tensor_tensor(res[i][:], su[i][:], su_at[i][:], ALU.add)
+            nc.sync.dma_start(out[P * i : P * (i + 1), :], res[i][:])
+
+        x2 = pick("x2", l_two, S)
+        w2g = [cast_plain("w2g0", w2_raw[0], scalar_copy)]
+        w2q = [quantize("w2q0", w2g[0][:], HALF)]
+        w2g.append(cast_plain("w2g1", w2_raw[1], scalar_copy))
+        w2q.append(quantize("w2q1", w2g[1][:], HALF))
+        x1 = pick("x1", l_offs, S)
+        w1g = [cast_plain("w1g0", w1_raw[0], scalar_copy)]
+        w1g.append(cast_plain("w1g1", w1_raw[1], vector_copy))
+        w1q = [quantize(f"w1q{h}", w1g[h][:], HALF) for h in range(2)]
+        for t in range(TILES):
+            d_tile(t, w2q[t // 2], x2)
+        for t in range(TILES):
+            y_tile(t, w1q[t // 2], x1, t < 2)
+        x3 = pick("x3", l_three, V)
+        cast_dealt(0, vector_copy)
+        cast_dealt(1, vector_copy)
+        w3q = quantize("w3q", w3_grouped[:].rearrange("p t m j -> p (t m j)"), H)
+        b_pair(0, w3q, x3, vector_copy)
+        b_pair(1, w3q, x3, vector_copy)
+        for t in range(TILES):
+            y_look(t, 0)
+        for t in range(TILES):
+            size_look(t, 0)
+        roots = []
+        for pair in range(2):
+            b_look(pair)
+            least_pair(pair)
+            ra_pair(pair)
+            roots.append(root_block(pair))
+        for t in range(TILES):
+            put(t)
+        on = [once_block(i, roots[i]) for i in range(2)]
+        zr = [z_block(i, on[i], roots[i]) for i in range(2)]
+        zg = [zg_block(i, zr[i], vector_copy) for i in range(2)]
+        zq = [zq_block(i, zg[i]) for i in range(2)]
+        for t in range(TILES):
+            size_look(t, 1)
+        for t in range(TILES):
+            z2_tile(t)
+        z2q = z2_quantize()
+        for t in range(TILES):
+            y_look(t, 1)
+        roots += [root_block(2), root_block(3)]
+        for i in range(2, 4):
+            on = once_block(i, roots[i])
+            zq.append(zq_block(i, zg_block(i, z_block(i, on, roots[i]), vector_copy)))
+            s_block(i - 2, zq[i - 2], True)
+            s_look(i - 2)
+            st_block(i - 2)
+        for i in range(4):
+            if i >= 2:
+                s_block(i, zq[i], True)
+                s_look(i)
+                st_block(i)
+            st_look(i, gather_s if i < 1 else gather_v)
+            su_block(i)
+            su_look(i)
+            out_block(i)

@@ -53,29 +53,33 @@ def tile_picked_twknormbkminthree_none_p_kernel(
         xw = sb("xw", [P, T], U32)
         nc.sync.dma_start(xw[:].bitcast(I32), x_words[0].rearrange("p n t -> p (n t)").bitcast(I32))
         for q in range(4):
-            nc.scalar.dma_start(xs[32 * q : 32 * q + 4, :].bitcast(I32), x_scales[0, 4 * q : 4 * q + 4, :].bitcast(I32))
-        ga_sb = sb("ga_sb", [P, TILES], F32)
-        with nc.allow_non_contiguous_dma(reason="one value a partition"):
-            nc.gpsimd.dma_start(ga_sb[:], ga.rearrange("(t p) o -> p (t o)", p=P))
-        gb_sb = sb("gb_sb", [P, TILES], F32)
-        nc.gpsimd.dma_start(gb_sb[:], gb.rearrange("(p t) o -> p (t o)", t=TILES))
+            nc.sync.dma_start(xs[32 * q : 32 * q + 4, :].bitcast(I32), x_scales[0, 4 * q : 4 * q + 4, :].bitcast(I32))
+        l_three = load_list("l_three", three)
         w2_raw.append(load_weight_half("w2_raw0", w2, 0))
         w2_raw.append(load_weight_half("w2_raw1", w2, 1))
-        l_offs = load_list("l_offs", offs)
         w1_raw.append(load_weight_half("w1_raw0", w1, 0))
+        l_offs = load_list("l_offs", offs)
+        ga_sb = sb("ga_sb", [P, TILES], F32)
+        with nc.allow_non_contiguous_dma(reason="one value a partition"):
+            nc.sync.dma_start(ga_sb[:], ga.rearrange("(t p) o -> p (t o)", p=P))
         w1_raw.append(load_weight_half("w1_raw1", w1, 1))
-        l_three = load_list("l_three", three)
         w3_raw.append(load_weight_half("w3_raw0", w3, 0))
         w3_raw.append(load_weight_half("w3_raw1", w3, 1))
         l_n1 = load_list("l_n1", n1)
         l_n4 = load_list("l_n4", n4)
         l_n3 = load_list("l_n3", n3)
         l_n2 = load_list("l_n2", n2)
+        gb_sb = sb("gb_sb", [P, TILES], F32)
+        nc.sync.dma_start(gb_sb[:], gb.rearrange("(p t) o -> p (t o)", t=TILES))
         l_n5 = load_list("l_n5", n5)
         l_n6 = load_list("l_n6", n6)
         l_n7 = load_list("l_n7", n7)
         ident = sb("ident", [P, P], F32)
         make_identity(nc, ident[:])
+
+        warm = sb("warm", [P, 2], F32)
+        nc.gpsimd.memset(warm[:, 0:1], 1.0)
+        nc.scalar.activation(warm[:, 1:2], warm[:, 0:1], ACT.Abs_reciprocal_sqrt)
 
         scalar_copy, vector_copy = nc.scalar.copy, nc.vector.tensor_copy
 
@@ -105,6 +109,23 @@ def tile_picked_twknormbkminthree_none_p_kernel(
                 raw[:].rearrange("p j (c i) -> p c j i", i=4),
             )
             return grouped
+
+        def cast_plain_g(name, raw):
+            grouped = sb(name, [P, HALF * PACK], BF16)
+            nc.gpsimd.tensor_scalar(
+                grouped[:].rearrange("p (c j) -> p c j", j=PACK), raw[:].rearrange("p j c -> p c j"), 1.0, 0.0, ALU.mult, ALU.add
+            )
+            return grouped
+
+        def cast_dealt_g(h):
+            nc.gpsimd.tensor_scalar(
+                w3_grouped[:, :, 64 * h : 64 * (h + 1), :],
+                w3_raw[h][:].rearrange("p j (m t) -> p t m j", t=TILES),
+                1.0,
+                0.0,
+                ALU.mult,
+                ALU.add,
+            )
 
         def cast_dealt(h, copy):
             copy(
@@ -141,12 +162,12 @@ def tile_picked_twknormbkminthree_none_p_kernel(
             [(pa, old)[t % 2][t // 2][:, 0:HALF] for t in range(TILES)],
         ]
         y = [sb(f"y{t}", [P, S], F32) for t in range(TILES)]
+        z_late = sb("z_late", [P, 2 * H], BF16)
+        z_all = [sb(f"z_rows{i}", [P, H], BF16)[:] for i in range(2)] + [z_late[:, H * e : H * (e + 1)] for e in range(2)]
         y_at = [
             [sb(f"y_at{t}", [P, HALF], F32)[:] for t in range(TILES)],
-            [sb(f"y_late{t}", [P, HALF], F32)[:] for t in range(2)] + [late[1][:, HALF * e : HALF * (e + 1)] for e in range(2)],
+            [sb(f"y_late{t}", [P, HALF], F32)[:] for t in range(2)] + [z_all[e].bitcast(F32) for e in range(2)],
         ]
-        once_late = sb("once_late", [P, 2 * H], F32)
-        z2_grouped = once_late[:, HALF : HALF + H].bitcast(BF16)
         staged = sb("staged", [P, TILES * V], BF16)
         z2_rows = staged[:].rearrange("p (t v) -> p t v", t=TILES)
 
@@ -190,14 +211,15 @@ def tile_picked_twknormbkminthree_none_p_kernel(
             nc.vector.tensor_scalar(z2_rows[:, t, :], b[t][:], gb_sb[:, t : t + 1], None, ALU.mult)
 
         def z2_quantize():
+            z2_grouped = z_late[:]
             nc.vector.tensor_copy(
                 z2_grouped.rearrange("p (c i t) -> p c t i", i=4, t=PACK),
                 z2_rows.rearrange("p t (c i) -> p c t i", i=4),
             )
             return quantize("z2q", z2_grouped, V)
 
-        def size_look(t, h):
-            gather_v(size_at[h][t], size[t], l_n2[:, 16 * h : 16 * (h + 1)])
+        def size_look(t, h, gather):
+            gather(size_at[h][t], size[t], l_n2[:, 16 * h : 16 * (h + 1)])
 
         def y_look(t, h):
             gather_s(y_at[h][t], y[t], l_n1[:, 16 * h : 16 * (h + 1)], scale=-1.0)
@@ -223,9 +245,9 @@ def tile_picked_twknormbkminthree_none_p_kernel(
             return root
 
         def once_block(i, root):
-            diff = bank(f"diff{i}", 4 + i)
+            diff = bank(f"diff{i}", 4 + i if i < 2 else i - 2)
             add_transposed(diff, y_at[i // 2], y, i)
-            once = once_late[:, H * (i - 2) : H * (i - 1)] if i >= 2 else sb(f"once{i}", [P, H], F32)[:]
+            once = sb(f"once{i}", [P, H], F32)[:]
             nc.vector.tensor_tensor(
                 once.rearrange(DEALT, u=2, e=2),
                 diff[:].rearrange(PLAIN, u=2, e=2),
@@ -234,14 +256,28 @@ def tile_picked_twknormbkminthree_none_p_kernel(
             )
             return once
 
+        def z_block_squared(i, root):
+            diff = bank(f"diff{i}", 4 + i if i < 2 else i - 2)
+            add_transposed(diff, y_at[i // 2], y, i)
+            inverse = sb(f"once{i}", [P, H], F32)[:]
+            nc.scalar.activation(inverse, root[:], ACT.Square)
+            z_rows = z_all[i]
+            nc.vector.tensor_tensor(
+                z_rows.rearrange(DEALT, u=2, e=2),
+                diff[:].rearrange(PLAIN, u=2, e=2),
+                inverse.rearrange(DEALT, u=2, e=2),
+                ALU.mult,
+            )
+            return z_rows
+
         def z_block(i, once, root):
-            z_rows = sb(f"z_rows{i}", [P, H], BF16)
-            nc.vector.tensor_tensor(z_rows[:], once, root[:], ALU.mult)
+            z_rows = z_all[i]
+            nc.vector.tensor_tensor(z_rows, once, root[:], ALU.mult)
             return z_rows
 
         def zg_block(i, z_rows, copy):
             turned = bank(f"turned{i}", 4 + (i + 2) % 4)
-            words = z_rows[:].bitcast(F32)
+            words = z_rows.bitcast(F32)
             for u in range(2):
                 nc.tensor.transpose(turned[:, P * u : P * (u + 1)], words[:, P * u : P * (u + 1)], ident[:])
             z_grouped = staged[:, H * i : H * (i + 1)] if i < 2 else sb(f"z_grouped{i}", [P, H], BF16)[:]
@@ -255,7 +291,7 @@ def tile_picked_twknormbkminthree_none_p_kernel(
             return quantize(f"zq{i}", z_grouped, P)
 
         def s_block(i, zq, on_scalar):
-            acc = bank(f"s_acc{i}", i)
+            acc = bank(f"s_acc{i}", 6 + i if i < 2 else i)
             mm(acc[:, 0:V], zq, 0, z2q, V)
             if on_scalar:
                 nc.scalar.activation(s[i][:], acc[:, 0:V], ACT.Copy, scale=0.0625)
@@ -301,7 +337,7 @@ def tile_picked_twknormbkminthree_none_p_kernel(
         for t in range(TILES):
             d_tile(t, w2q[t // 2], x2)
         for t in range(TILES):
-            y_tile(t, w1q[t // 2], x1, t < 2)
+            y_tile(t, w1q[t // 2], x1, t < 3)
         x3 = pick("x3", l_three, V)
         cast_dealt(0, vector_copy)
         cast_dealt(1, vector_copy)
@@ -311,7 +347,7 @@ def tile_picked_twknormbkminthree_none_p_kernel(
         for t in range(TILES):
             y_look(t, 0)
         for t in range(TILES):
-            size_look(t, 0)
+            size_look(t, 0, gather_v)
         roots = []
         for pair in range(2):
             b_look(pair)
@@ -325,7 +361,7 @@ def tile_picked_twknormbkminthree_none_p_kernel(
         zg = [zg_block(i, zr[i], vector_copy) for i in range(2)]
         zq = [zq_block(i, zg[i]) for i in range(2)]
         for t in range(TILES):
-            size_look(t, 1)
+            size_look(t, 1, gather_v)
         for t in range(TILES):
             z2_tile(t)
         z2q = z2_quantize()
@@ -333,17 +369,17 @@ def tile_picked_twknormbkminthree_none_p_kernel(
             y_look(t, 1)
         roots += [root_block(2), root_block(3)]
         for i in range(2, 4):
-            on = once_block(i, roots[i])
-            zq.append(zq_block(i, zg_block(i, z_block(i, on, roots[i]), vector_copy)))
-            s_block(i - 2, zq[i - 2], True)
-            s_look(i - 2)
-            st_block(i - 2)
+            zr.append(z_block_squared(i, roots[i]))
+        for i in range(2, 4):
+            zq.append(zq_block(i, zg_block(i, zr[i], vector_copy)))
         for i in range(4):
-            if i >= 2:
-                s_block(i, zq[i], True)
-                s_look(i)
-                st_block(i)
+            s_block(i, zq[i], True)
+        for i in range(4):
+            s_look(i)
+            st_block(i)
+        for i in range(4):
             st_look(i, gather_s if i < 1 else gather_v)
             su_block(i)
+        for i in range(4):
             su_look(i)
             out_block(i)

@@ -19,7 +19,18 @@ ALU = mybir.AluOpType
 P = 128
 PACK = 4
 TILES = H // P
+BLOCKS = S // P
 HALF = 256
+BANK = 512
+QUADRANT = 32
+ENTRIES = 16
+
+FIRST_SQUARE_ON_SCALAR = 2
+FIRST_TURN_ON_SCALAR = 1
+FIRST_N6_ON_SCALAR = 3
+
+PLAIN = "p (m u e) -> p u m e"
+DEALT = "p (u m e) -> p u m e"
 
 
 def tile_picked_twknormbkminthree_none_p_kernel(
@@ -30,50 +41,49 @@ def tile_picked_twknormbkminthree_none_p_kernel(
         keep = ctx.enter_context(tc.tile_pool(name="keep", bufs=1))
         psum = ctx.enter_context(tc.psum_pool(name="psum", bufs=1))
 
-        def sb(name, shape, dtype, tag=None):
-            return keep.tile(shape, dtype, name=name, tag=tag or name, align_bytes=64)
+        def sb(name, shape, dtype):
+            return keep.tile(shape, dtype, name=name, align_bytes=64)
 
         def bank(name, number):
-            return psum.tile([P, 512], F32, name=name, tag=f"bank{number}")
+            return psum.tile([P, BANK], F32, name=name, tag=f"bank{number}")
 
         def load_list(name, src):
-            t = sb(name, list(src.shape), U16)
-            nc.sync.dma_start(t[:], src)
-            return t
+            tile = sb(name, list(src.shape), U16)
+            nc.sync.dma_start(tile[:], src)
+            return tile
 
-        def load_weight_half(name, w, h):
-            raw = sb(name, [P, PACK, HALF], F32)
-            nc.sync.dma_start(raw[:], w[:, HALF * h : HALF * (h + 1)].rearrange("(p j) c -> p j c", j=PACK))
-            return raw
+        def load_weight(name, w):
+            halves = [sb(f"{name}{h}", [P, PACK, HALF], F32) for h in range(2)]
+            for h in range(2):
+                nc.sync.dma_start(halves[h][:], w[:, HALF * h : HALF * (h + 1)].rearrange("(p j) c -> p j c", j=PACK))
+            return halves
 
-        xs = sb("xs", [P, T], U8)
-        nc.gpsimd.memset(xs[:].bitcast(I32), 0)
-        w1_raw, w2_raw, w3_raw = [], [], []
-        l_two = load_list("l_two", two)
-        xw = sb("xw", [P, T], U32)
-        nc.sync.dma_start(xw[:].bitcast(I32), x_words[0].rearrange("p n t -> p (n t)").bitcast(I32))
-        for q in range(4):
-            nc.sync.dma_start(xs[32 * q : 32 * q + 4, :].bitcast(I32), x_scales[0, 4 * q : 4 * q + 4, :].bitcast(I32))
-        l_three = load_list("l_three", three)
-        w2_raw.append(load_weight_half("w2_raw0", w2, 0))
-        w2_raw.append(load_weight_half("w2_raw1", w2, 1))
-        w1_raw.append(load_weight_half("w1_raw0", w1, 0))
-        l_offs = load_list("l_offs", offs)
-        ga_sb = sb("ga_sb", [P, TILES], F32)
-        with nc.allow_non_contiguous_dma(reason="one value a partition"):
-            nc.sync.dma_start(ga_sb[:], ga.rearrange("(t p) o -> p (t o)", p=P))
-        w1_raw.append(load_weight_half("w1_raw1", w1, 1))
-        w3_raw.append(load_weight_half("w3_raw0", w3, 0))
-        w3_raw.append(load_weight_half("w3_raw1", w3, 1))
-        l_n1 = load_list("l_n1", n1)
-        l_n4 = load_list("l_n4", n4)
-        l_n3 = load_list("l_n3", n3)
-        l_n2 = load_list("l_n2", n2)
-        gb_sb = sb("gb_sb", [P, TILES], F32)
-        nc.sync.dma_start(gb_sb[:], gb.rearrange("(p t) o -> p (t o)", t=TILES))
-        l_n5 = load_list("l_n5", n5)
-        l_n6 = load_list("l_n6", n6)
-        l_n7 = load_list("l_n7", n7)
+        table_scales = sb("table_scales", [P, T], U8)
+        nc.gpsimd.memset(table_scales[:].bitcast(I32), 0)
+        three_list = load_list("three_list", three)
+        table_words = sb("table_words", [P, T], U32)
+        nc.sync.dma_start(table_words[:].bitcast(I32), x_words[0].rearrange("p n t -> p (n t)").bitcast(I32))
+        two_list = load_list("two_list", two)
+        for q in range(P // QUADRANT):
+            nc.sync.dma_start(
+                table_scales[QUADRANT * q : QUADRANT * q + 4, :].bitcast(I32), x_scales[0, 4 * q : 4 * q + 4, :].bitcast(I32)
+            )
+        w3_raw = load_weight("w3_raw", w3)
+        w2_raw = load_weight("w2_raw", w2)
+        n4_list = load_list("n4_list", n4)
+        n3_list = load_list("n3_list", n3)
+        offs_list = load_list("offs_list", offs)
+        w1_raw = load_weight("w1_raw", w1)
+        ga_cols = sb("ga_cols", [P, TILES], F32)
+        with nc.allow_non_contiguous_dma(reason="one value of ga for each partition and tile"):
+            nc.sync.dma_start(ga_cols[:], ga.rearrange("(t p) o -> p (t o)", p=P))
+        n1_list = load_list("n1_list", n1)
+        n2_list = load_list("n2_list", n2)
+        gb_cols = sb("gb_cols", [P, TILES], F32)
+        nc.sync.dma_start(gb_cols[:], gb.rearrange("(p t) o -> p (t o)", t=TILES))
+        n5_list = load_list("n5_list", n5)
+        n6_list = load_list("n6_list", n6)
+        n7_list = load_list("n7_list", n7)
         ident = sb("ident", [P, P], F32)
         make_identity(nc, ident[:])
 
@@ -81,305 +91,194 @@ def tile_picked_twknormbkminthree_none_p_kernel(
         nc.gpsimd.memset(warm[:, 0:1], 1.0)
         nc.scalar.activation(warm[:, 1:2], warm[:, 0:1], ACT.Abs_reciprocal_sqrt)
 
-        scalar_copy, vector_copy = nc.scalar.copy, nc.vector.tensor_copy
-
-        def pick_words(name, lst, n, tag=None):
-            words = sb(name + "_words", [P, n], U32, tag)
-            nc.vector.tensor_copy(words[:], xw[:].indirect(lst[:]))
-            return words
-
-        def pick_scales(name, lst, n, tag=None):
-            scales = sb(name + "_scales", [P, n], U8, tag)
-            nc.vector.tensor_copy(scales[:], xs[:].indirect(lst[:]))
-            return scales
-
-        def pick(name, lst, n):
-            return pick_words(name, lst, n), pick_scales(name, lst, n)
+        def pick(name, entries, n):
+            words = sb(name + "_words", [P, n], U32)
+            nc.vector.tensor_copy(words[:], table_words[:].indirect(entries[:]))
+            scales = sb(name + "_scales", [P, n], U8)
+            nc.vector.tensor_copy(scales[:], table_scales[:].indirect(entries[:]))
+            return words, scales
 
         def quantize(name, grouped, n):
             codes = sb(name + "_codes", [P, n], U32)
-            scales = sb(name + "_sc", [P, n], U8)
+            scales = sb(name + "_planes", [P, n], U8)
             nc.vector.quantize_mx(out=codes[:].bitcast(FP8X4), scales=scales[:], in_=grouped)
             return codes, scales
 
-        def cast_plain(name, raw, copy):
+        def side_by_side(copy, name, rows):
             grouped = sb(name, [P, HALF * PACK], BF16)
-            copy(
-                grouped[:].rearrange("p (c i j) -> p c j i", i=4, j=PACK),
-                raw[:].rearrange("p j (c i) -> p c j i", i=4),
-            )
+            copy(grouped[:].rearrange("p (c i j) -> p c j i", i=4, j=PACK), rows.rearrange("p j (c i) -> p c j i", i=4))
             return grouped
 
-        def cast_plain_g(name, raw):
-            grouped = sb(name, [P, HALF * PACK], BF16)
-            nc.gpsimd.tensor_scalar(
-                grouped[:].rearrange("p (c j) -> p c j", j=PACK), raw[:].rearrange("p j c -> p c j"), 1.0, 0.0, ALU.mult, ALU.add
-            )
-            return grouped
-
-        def cast_dealt_g(h):
-            nc.gpsimd.tensor_scalar(
-                w3_grouped[:, :, 64 * h : 64 * (h + 1), :],
-                w3_raw[h][:].rearrange("p j (m t) -> p t m j", t=TILES),
-                1.0,
-                0.0,
-                ALU.mult,
-                ALU.add,
-            )
-
-        def cast_dealt(h, copy):
-            copy(
-                w3_grouped[:, :, 64 * h : 64 * (h + 1), :].rearrange("p t m j -> p m j t"),
-                w3_raw[h][:].rearrange("p j (m t) -> p m j t", t=TILES),
-            )
-
-        def mm(dst, lhs, m0, rhs, n):
+        def product(dst, stationary, first, moving):
             nc.tensor.matmul_mx(
                 out=dst,
-                lhsT=lhs[0][:, m0 : m0 + P].bitcast(FP8X4),
-                lhsT_scale=lhs[1][:, m0 : m0 + P],
-                rhs=rhs[0][:, 0:n].bitcast(FP8X4),
-                rhs_scale=rhs[1][:, 0:n],
+                lhsT=stationary[0][:, first : first + P].bitcast(FP8X4),
+                lhsT_scale=stationary[1][:, first : first + P],
+                rhs=moving[0][:].bitcast(FP8X4),
+                rhs_scale=moving[1][:],
                 start=True,
                 stop=True,
             )
 
-        def gather_s(dst, window, lst, scale=1.0):
-            nc.scalar.activation(dst, window[:].indirect(lst), ACT.Copy, scale=scale)
+        def look_scalar(dst, window, entries, scale=1.0):
+            nc.scalar.activation(dst, window[:].indirect(entries), ACT.Copy, scale=scale)
 
-        def gather_v(dst, window, lst):
-            nc.vector.tensor_copy(dst, window[:].indirect(lst))
+        def look_vector(dst, window, entries):
+            nc.vector.tensor_copy(dst, window[:].indirect(entries))
 
+        def half_of(entries, h):
+            return entries[:, HALF // ENTRIES * h : HALF // ENTRIES * (h + 1)]
+
+        def open_sum(name, number, plain, i):
+            dst = bank(name, number)
+            for t in range(TILES):
+                nc.tensor.matmul(
+                    dst[:, P * t : P * (t + 1)], plain[t][:, P * i : P * (i + 1)], ident[:], start=t == 0, stop=False, is_transpose=True
+                )
+            return dst
+
+        def close_sum(dst, looked, i):
+            for t in range(TILES):
+                nc.tensor.matmul(
+                    dst[:, P * t : P * (t + 1)],
+                    looked[t][:, P * (i % 2) : P * (i % 2 + 1)],
+                    ident[:],
+                    start=False,
+                    stop=t == TILES - 1,
+                    is_transpose=True,
+                )
+
+
+        x_three = pick("x_three", three_list, V)
         w3_grouped = sb("w3_grouped", [P, TILES, P, PACK], BF16)
+        for h in range(2):
+            nc.scalar.copy(
+                w3_grouped[:, :, P // 2 * h : P // 2 * (h + 1), :].rearrange("p t m j -> p m j t"),
+                w3_raw[h][:].rearrange("p j (m t) -> p m j t", t=TILES),
+            )
+        w3_mx = quantize("w3", w3_grouped[:].rearrange("p t m j -> p (t m j)"), H)
         b = [sb(f"b{t}", [P, V], F32) for t in range(TILES)]
-        pa = [sb(f"pa{pair}", [P, 2 * W], F32) for pair in range(2)]
-        old = [sb(f"old{pair}", [P, 2 * W], F32) for pair in range(2)]
-        late = [sb(f"late{pair}", [P, 2 * HALF], F32) for pair in range(2)]
-        ra = [late[pair][:, 0 : 2 * W] for pair in range(2)]
-        size = [sb(f"size{t}", [P, S], F32) for t in range(TILES)]
-        size_at = [
-            [sb(f"size_at{t}", [P, HALF], F32)[:] for t in range(TILES)],
-            [(pa, old)[t % 2][t // 2][:, 0:HALF] for t in range(TILES)],
-        ]
-        y = [sb(f"y{t}", [P, S], F32) for t in range(TILES)]
-        z_late = sb("z_late", [P, 2 * H], BF16)
-        z_all = [sb(f"z_rows{i}", [P, H], BF16)[:] for i in range(2)] + [z_late[:, H * e : H * (e + 1)] for e in range(2)]
-        y_at = [
-            [sb(f"y_at{t}", [P, HALF], F32)[:] for t in range(TILES)],
-            [sb(f"y_late{t}", [P, HALF], F32)[:] for t in range(2)] + [z_all[e].bitcast(F32) for e in range(2)],
-        ]
-        staged = sb("staged", [P, TILES * V], BF16)
-        z2_rows = staged[:].rearrange("p (t v) -> p t v", t=TILES)
-
-        def d_tile(t, wq, xq):
-            acc = bank(f"d_acc{t}", t)
-            mm(acc[:], wq, P * (t % 2), xq, S)
-            nc.scalar.activation(size[t][:], acc[:], ACT.Abs)
-
-        def y_tile(t, wq, xq, on_scalar):
-            acc = bank(f"y_acc{t}", 4 + t)
-            mm(acc[:], wq, P * (t % 2), xq, S)
-            if on_scalar:
-                nc.scalar.activation(y[t][:], acc[:], ACT.Copy, scale=ga_sb[:, t : t + 1])
-            else:
-                nc.vector.tensor_scalar(y[t][:], acc[:], ga_sb[:, t : t + 1], None, ALU.mult)
-
-        def b_pair(pair, wq, xq, copy):
-            acc = bank(f"b_acc{pair}", pair)
+        for pair, copy in enumerate((nc.scalar.copy, nc.vector.tensor_copy)):
+            acc = bank(f"b_acc{pair}", 4 + pair)
             for e in range(2):
-                mm(acc[:, V * e : V * (e + 1)], wq, P * (2 * pair + e), xq, V)
+                product(acc[:, V * e : V * (e + 1)], w3_mx, P * (2 * pair + e), x_three)
             for e in range(2):
                 copy(b[2 * pair + e][:], acc[:, V * e : V * (e + 1)])
 
-        def b_look(pair):
+        x_two = pick("x_two", two_list, S)
+        w2_grouped = [
+            side_by_side(copy, f"w2_grouped{h}", w2_raw[h][:]) for h, copy in enumerate((nc.scalar.copy, nc.vector.tensor_copy))
+        ]
+        w2_mx = [quantize(f"w2_{h}", w2_grouped[h][:], HALF) for h in range(2)]
+
+        ra = []
+        for pair in range(2):
+            pa, old, least = [sb(f"{name}{pair}", [P, 2 * W], F32) for name in ("pa", "old", "least")]
+            ra.append(sb(f"ra{pair}", [P, 2 * W], F32))
             for e in range(2):
-                gather_s(pa[pair][:, W * e : W * (e + 1)], b[2 * pair + e], l_n4[:])
-                gather_s(old[pair][:, W * e : W * (e + 1)], b[2 * pair + e], l_n3[:])
+                look_scalar(pa[:, W * e : W * (e + 1)], b[2 * pair + e], n4_list[:])
+                look_scalar(old[:, W * e : W * (e + 1)], b[2 * pair + e], n3_list[:])
+            nc.vector.tensor_tensor(least[:], pa[:], old[:], ALU.min)
+            nc.vector.scalar_tensor_tensor(ra[pair][:], pa[:], -0.5, least[:], ALU.mult, ALU.add)
 
-        least = [sb(f"least{pair}", [P, 2 * W], F32) for pair in range(2)]
+        size = [sb(f"size{t}", [P, S], F32) for t in range(TILES)]
+        for t in range(TILES):
+            acc = bank(f"d_acc{t}", t)
+            product(acc[:], w2_mx[t // 2], P * (t % 2), x_two)
+            nc.scalar.activation(size[t][:], acc[:], ACT.Abs)
+        totals = [open_sum(f"total{i}", 4 + i, size, i) for i in range(BLOCKS)]
+        for t in range(TILES):
+            nc.scalar.activation(b[t][:].indirect(n3_list[:]), ra[t // 2][:, W * (t % 2) : W * (t % 2 + 1)], ACT.Copy)
 
-        def least_pair(pair):
-            nc.vector.tensor_tensor(least[pair][:], pa[pair][:], old[pair][:], ALU.min)
+        x_offs = pick("x_offs", offs_list, S)
+        w1_grouped = [side_by_side(nc.vector.tensor_copy, f"w1_grouped{h}", w1_raw[h][:]) for h in range(2)]
+        w1_mx = [quantize(f"w1_{h}", w1_grouped[h][:], HALF) for h in range(2)]
+        y = [sb(f"y{t}", [P, S], F32) for t in range(TILES)]
+        for t in range(TILES):
+            acc = bank(f"y_acc{t}", t)
+            product(acc[:], w1_mx[t // 2], P * (t % 2), x_offs)
+            nc.vector.tensor_scalar(y[t][:], acc[:], ga_cols[:, t : t + 1], None, ALU.mult)
+        diffs = [open_sum(f"diff{i}", i, y, i) for i in range(BLOCKS)]
 
-        def ra_pair(pair):
-            nc.vector.scalar_tensor_tensor(ra[pair], pa[pair][:], -0.5, least[pair][:], ALU.mult, ALU.add)
+        y_at = [sb(f"y_at{t}", [P, HALF], F32) for t in range(TILES)]
+        size_first = sb("size_first", [P, TILES, HALF], F32)
+        size_at = [
+            [size_first[:, t, :] for t in range(TILES)],
+            [sb(f"size_second{t}", [P, HALF], F32)[:] for t in range(TILES)],
+        ]
 
-        def put(t):
-            nc.scalar.activation(b[t][:].indirect(l_n3[:]), ra[t // 2][:, W * (t % 2) : W * (t % 2 + 1)], ACT.Copy)
-
-        def z2_tile(t):
-            nc.vector.tensor_scalar(z2_rows[:, t, :], b[t][:], gb_sb[:, t : t + 1], None, ALU.mult)
-
-        def z2_quantize():
-            z2_grouped = z_late[:]
-            nc.vector.tensor_copy(
-                z2_grouped.rearrange("p (c i t) -> p c t i", i=4, t=PACK),
-                z2_rows.rearrange("p t (c i) -> p c t i", i=4),
-            )
-            return quantize("z2q", z2_grouped, V)
-
-        def size_look(t, h, gather):
-            gather(size_at[h][t], size[t], l_n2[:, 16 * h : 16 * (h + 1)])
-
-        def y_look(t, h):
-            gather_s(y_at[h][t], y[t], l_n1[:, 16 * h : 16 * (h + 1)], scale=-1.0)
-
-        def add_transposed(dst, first, second, i):
-            cols = slice(P * i, P * (i + 1))
-            in_half = slice(P * (i % 2), P * (i % 2 + 1))
+        def look_up_half(h):
             for t in range(TILES):
-                o = dst[:, P * t : P * (t + 1)]
-                nc.tensor.matmul(o, first[t][:, in_half], ident[:], start=True, stop=False, is_transpose=True)
-                nc.tensor.matmul(o, second[t][:, cols], ident[:], start=False, stop=True, is_transpose=True)
+                look_scalar(y_at[t][:], y[t], half_of(n1_list, h), scale=-1.0)
+                look_vector(size_at[h][t], size[t], half_of(n2_list, h))
+            for i in (2 * h, 2 * h + 1):
+                close_sum(totals[i], size_at[h], i)
 
-        DEALT = "p (u m e) -> p u m e"
-        PLAIN = "p (m u e) -> p u m e"
+        look_up_half(0)
 
-        def root_block(i):
-            total = bank(f"total{i}", 2 + i % 2)
-            add_transposed(total, size_at[i // 2], size, i)
-            root = sb(f"root{i}", [P, H], F32)
-            nc.scalar.activation(
-                root[:].rearrange(DEALT, u=2, e=2), total[:].rearrange(PLAIN, u=2, e=2), ACT.Abs_reciprocal_sqrt, bias=0.5
-            )
-            return root
+        z2_rows = size_first[:].bitcast(BF16)[:, :, 0:V]
+        for t in range(TILES):
+            nc.vector.tensor_scalar(z2_rows[:, t, :], b[t][:], gb_cols[:, t : t + 1], None, ALU.mult)
+        z2_mx = quantize("z2", side_by_side(nc.vector.tensor_copy, "z2_grouped", z2_rows)[:], V)
 
-        def once_block(i, root):
-            diff = bank(f"diff{i}", 4 + i if i < 2 else i - 2)
-            add_transposed(diff, y_at[i // 2], y, i)
-            once = sb(f"once{i}", [P, H], F32)[:]
-            nc.vector.tensor_tensor(
-                once.rearrange(DEALT, u=2, e=2),
-                diff[:].rearrange(PLAIN, u=2, e=2),
-                root[:].rearrange(DEALT, u=2, e=2),
-                ALU.mult,
-            )
-            return once
+        root = [sb(f"root{i}", [P, H], F32) for i in range(BLOCKS)]
 
-        def z_block_squared(i, root):
-            diff = bank(f"diff{i}", 4 + i if i < 2 else i - 2)
-            add_transposed(diff, y_at[i // 2], y, i)
-            inverse = sb(f"once{i}", [P, H], F32)[:]
-            nc.scalar.activation(inverse, root[:], ACT.Square)
-            z_rows = z_all[i]
-            nc.vector.tensor_tensor(
-                z_rows.rearrange(DEALT, u=2, e=2),
-                diff[:].rearrange(PLAIN, u=2, e=2),
-                inverse.rearrange(DEALT, u=2, e=2),
-                ALU.mult,
-            )
-            return z_rows
+        def z_words(i):
+            close_sum(diffs[i], y_at, i)
+            diff = diffs[i][:].rearrange(PLAIN, u=2, e=2)
+            between = sb(f"between{i}", [P, H], F32)
+            z = sb(f"z{i}", [P, H], BF16)
+            if i >= FIRST_SQUARE_ON_SCALAR:
+                nc.scalar.activation(between[:], root[i][:], ACT.Square)
+                nc.vector.tensor_tensor(z[:].rearrange(DEALT, u=2, e=2), diff, between[:].rearrange(DEALT, u=2, e=2), ALU.mult)
+            else:
+                nc.vector.tensor_tensor(between[:].rearrange(DEALT, u=2, e=2), diff, root[i][:].rearrange(DEALT, u=2, e=2), ALU.mult)
+                nc.vector.tensor_tensor(z[:], between[:], root[i][:], ALU.mult)
+            return z[:].bitcast(F32)
 
-        def z_block(i, once, root):
-            z_rows = z_all[i]
-            nc.vector.tensor_tensor(z_rows, once, root[:], ALU.mult)
-            return z_rows
-
-        def zg_block(i, z_rows, copy):
-            turned = bank(f"turned{i}", 4 + (i + 2) % 4)
-            words = z_rows.bitcast(F32)
+        def z_quantized(i, words):
+            turned = bank(f"turned{i}", 4 + i)
             for u in range(2):
                 nc.tensor.transpose(turned[:, P * u : P * (u + 1)], words[:, P * u : P * (u + 1)], ident[:])
-            z_grouped = staged[:, H * i : H * (i + 1)] if i < 2 else sb(f"z_grouped{i}", [P, H], BF16)[:]
+            grouped = sb(f"z_grouped{i}", [P, P * PACK], BF16)
+            copy = nc.scalar.copy if i >= FIRST_TURN_ON_SCALAR else nc.vector.tensor_copy
             copy(
-                z_grouped.bitcast(F32).rearrange("p (r u) -> p r u", u=2),
+                grouped[:].bitcast(F32).rearrange("p (r u) -> p r u", u=2),
                 turned[:, 0 : 2 * P].rearrange("p (u r) -> p r u", u=2),
             )
-            return z_grouped
+            return quantize(f"z_{i}", grouped[:], P)
 
-        def zq_block(i, z_grouped):
-            return quantize(f"zq{i}", z_grouped, P)
+        z_mx = []
+        for h in range(2):
+            blocks = (2 * h, 2 * h + 1)
+            if h == 1:
+                look_up_half(1)
+            for i in blocks:
+                nc.scalar.activation(
+                    root[i][:].rearrange(DEALT, u=2, e=2),
+                    totals[i][:].rearrange(PLAIN, u=2, e=2),
+                    ACT.Abs_reciprocal_sqrt,
+                    bias=0.5,
+                )
+            words = [z_words(i) for i in blocks]
+            z_mx.extend(z_quantized(i, words[i % 2]) for i in blocks)
 
-        def s_block(i, zq, on_scalar):
-            acc = bank(f"s_acc{i}", 6 + i if i < 2 else i)
-            mm(acc[:, 0:V], zq, 0, z2q, V)
-            if on_scalar:
-                nc.scalar.activation(s[i][:], acc[:, 0:V], ACT.Copy, scale=0.0625)
-            else:
-                nc.vector.tensor_scalar(s[i][:], acc[:, 0:V], 0.0625, None, ALU.mult)
-
-        s, s_at, st, st_at, su, su_at, res = [
-            [sb(f"{name}{i}", [P, V], F32) for i in range(4)] for name in ("s", "s_at", "st", "st_at", "su", "su_at", "res")
+        s, st, su = size, y, root
+        s_at, st_at, su_at, result = [
+            [sb(f"{name}{i}", [P, V], F32) for i in range(BLOCKS)] for name in ("s_at", "st_at", "su_at", "result")
         ]
-        parts = [(slice(P * h, P * (h + 1)), slice(8 * h, 8 * (h + 1))) for h in range(2)]
-
-        def s_look(i):
-            for cols, entries in parts:
-                gather_s(s_at[i][:, cols], s[i], l_n5[:, entries])
-
-        def st_block(i):
-            nc.vector.tensor_tensor(st[i][:], s[i][:], s_at[i][:], ALU.subtract)
-
-        def st_look(i, gather):
-            for cols, entries in parts:
-                gather(st_at[i][:, cols], st[i], l_n6[:, entries])
-
-        def su_block(i):
-            nc.vector.tensor_tensor(su[i][:], st[i][:], st_at[i][:], ALU.max)
-
-        def su_look(i):
-            for cols, entries in parts:
-                gather_s(su_at[i][:, cols], su[i], l_n7[:, entries], scale=0.5)
-
-        def out_block(i):
-            nc.vector.tensor_tensor(res[i][:], su[i][:], su_at[i][:], ALU.add)
-            nc.sync.dma_start(out[P * i : P * (i + 1), :], res[i][:])
-
-        x2 = pick("x2", l_two, S)
-        w2g = [cast_plain("w2g0", w2_raw[0], scalar_copy)]
-        w2q = [quantize("w2q0", w2g[0][:], HALF)]
-        w2g.append(cast_plain("w2g1", w2_raw[1], scalar_copy))
-        w2q.append(quantize("w2q1", w2g[1][:], HALF))
-        x1 = pick("x1", l_offs, S)
-        w1g = [cast_plain("w1g0", w1_raw[0], scalar_copy)]
-        w1g.append(cast_plain("w1g1", w1_raw[1], vector_copy))
-        w1q = [quantize(f"w1q{h}", w1g[h][:], HALF) for h in range(2)]
-        for t in range(TILES):
-            d_tile(t, w2q[t // 2], x2)
-        for t in range(TILES):
-            y_tile(t, w1q[t // 2], x1, t < 3)
-        x3 = pick("x3", l_three, V)
-        cast_dealt(0, vector_copy)
-        cast_dealt(1, vector_copy)
-        w3q = quantize("w3q", w3_grouped[:].rearrange("p t m j -> p (t m j)"), H)
-        b_pair(0, w3q, x3, vector_copy)
-        b_pair(1, w3q, x3, vector_copy)
-        for t in range(TILES):
-            y_look(t, 0)
-        for t in range(TILES):
-            size_look(t, 0, gather_v)
-        roots = []
-        for pair in range(2):
-            b_look(pair)
-            least_pair(pair)
-            ra_pair(pair)
-            roots.append(root_block(pair))
-        for t in range(TILES):
-            put(t)
-        on = [once_block(i, roots[i]) for i in range(2)]
-        zr = [z_block(i, on[i], roots[i]) for i in range(2)]
-        zg = [zg_block(i, zr[i], vector_copy) for i in range(2)]
-        zq = [zq_block(i, zg[i]) for i in range(2)]
-        for t in range(TILES):
-            size_look(t, 1, gather_v)
-        for t in range(TILES):
-            z2_tile(t)
-        z2q = z2_quantize()
-        for t in range(TILES):
-            y_look(t, 1)
-        roots += [root_block(2), root_block(3)]
-        for i in range(2, 4):
-            zr.append(z_block_squared(i, roots[i]))
-        for i in range(2, 4):
-            zq.append(zq_block(i, zg_block(i, zr[i], vector_copy)))
-        for i in range(4):
-            s_block(i, zq[i], True)
-        for i in range(4):
-            s_look(i)
-            st_block(i)
-        for i in range(4):
-            st_look(i, gather_s if i < 1 else gather_v)
-            su_block(i)
-        for i in range(4):
-            su_look(i)
-            out_block(i)
+        for i in range(BLOCKS):
+            acc = bank(f"s_acc{i}", i)
+            product(acc[:, 0:V], z_mx[i], 0, z2_mx)
+            nc.scalar.activation(s[i][:, 0:V], acc[:, 0:V], ACT.Copy, scale=0.0625)
+        for i in range(BLOCKS):
+            look_scalar(s_at[i][:], s[i], n5_list[:])
+            nc.vector.tensor_tensor(st[i][:, 0:V], s[i][:, 0:V], s_at[i][:], ALU.subtract)
+        for i in range(BLOCKS):
+            look = look_scalar if i >= FIRST_N6_ON_SCALAR else look_vector
+            look(st_at[i][:], st[i], n6_list[:])
+            nc.vector.tensor_tensor(su[i][:, 0:V], st[i][:, 0:V], st_at[i][:], ALU.max)
+        for i in range(BLOCKS):
+            look_scalar(su_at[i][:], su[i], n7_list[:], scale=0.5)
+            nc.vector.tensor_tensor(result[i][:], su[i][:, 0:V], su_at[i][:], ALU.add)
+            nc.sync.dma_start(out[P * i : P * (i + 1), :], result[i][:])

@@ -74,11 +74,11 @@ def tile_picked_twknormbkminthree_none_p_kernel(
         n3_list = load_list("n3_list", n3)
         offs_list = load_list("offs_list", offs)
         w1_raw = load_weight("w1_raw", w1)
+        n2_list = load_list("n2_list", n2)
         ga_cols = sb("ga_cols", [P, TILES], F32)
         with nc.allow_non_contiguous_dma(reason="one value of ga for each partition and tile"):
             nc.sync.dma_start(ga_cols[:], ga.rearrange("(t p) o -> p (t o)", p=P))
         n1_list = load_list("n1_list", n1)
-        n2_list = load_list("n2_list", n2)
         gb_cols = sb("gb_cols", [P, TILES], F32)
         nc.sync.dma_start(gb_cols[:], gb.rearrange("(p t) o -> p (t o)", t=TILES))
         n5_list = load_list("n5_list", n5)
@@ -156,20 +156,29 @@ def tile_picked_twknormbkminthree_none_p_kernel(
                 w3_grouped[:, :, P // 2 * h : P // 2 * (h + 1), :].rearrange("p t m j -> p m j t"),
                 w3_raw[h][:].rearrange("p j (m t) -> p m j t", t=TILES),
             )
-        w3_mx = quantize("w3", w3_grouped[:].rearrange("p t m j -> p (t m j)"), H)
-        b = [sb(f"b{t}", [P, V], F32) for t in range(TILES)]
-        for pair, copy in enumerate((nc.scalar.copy, nc.vector.tensor_copy)):
-            acc = bank(f"b_acc{pair}", 4 + pair)
-            for e in range(2):
-                product(acc[:, V * e : V * (e + 1)], w3_mx, P * (2 * pair + e), x_three)
-            for e in range(2):
-                copy(b[2 * pair + e][:], acc[:, V * e : V * (e + 1)])
-
+        w3_mx = [
+            quantize(f"w3_{pair}", w3_grouped[:, 2 * pair : 2 * pair + 2].rearrange("p t m j -> p (t m j)"), HALF) for pair in range(2)
+        ]
         x_two = pick("x_two", two_list, S)
         w2_grouped = [
             side_by_side(copy, f"w2_grouped{h}", w2_raw[h][:]) for h, copy in enumerate((nc.scalar.copy, nc.vector.tensor_copy))
         ]
         w2_mx = [quantize(f"w2_{h}", w2_grouped[h][:], HALF) for h in range(2)]
+
+        b = [sb(f"b{t}", [P, V], F32) for t in range(TILES)]
+        for pair, copy in enumerate((nc.scalar.copy, nc.vector.tensor_copy)):
+            acc = bank(f"b_acc{pair}", 4 + pair)
+            for e in range(2):
+                product(acc[:, V * e : V * (e + 1)], w3_mx[pair], P * e, x_three)
+            for e in range(2):
+                copy(b[2 * pair + e][:], acc[:, V * e : V * (e + 1)])
+
+        size = [sb(f"size{t}", [P, S], F32) for t in range(TILES)]
+        for t in range(TILES):
+            acc = bank(f"d_acc{t}", t)
+            product(acc[:], w2_mx[t // 2], P * (t % 2), x_two)
+            nc.scalar.activation(size[t][:], acc[:], ACT.Abs)
+        totals = [open_sum(f"total{i}", 4 + i, size, i) for i in range(BLOCKS)]
 
         ra = []
         for pair in range(2):
@@ -180,13 +189,6 @@ def tile_picked_twknormbkminthree_none_p_kernel(
                 look_scalar(old[:, W * e : W * (e + 1)], b[2 * pair + e], n3_list[:])
             nc.vector.tensor_tensor(least[:], pa[:], old[:], ALU.min)
             nc.vector.scalar_tensor_tensor(ra[pair][:], pa[:], -0.5, least[:], ALU.mult, ALU.add)
-
-        size = [sb(f"size{t}", [P, S], F32) for t in range(TILES)]
-        for t in range(TILES):
-            acc = bank(f"d_acc{t}", t)
-            product(acc[:], w2_mx[t // 2], P * (t % 2), x_two)
-            nc.scalar.activation(size[t][:], acc[:], ACT.Abs)
-        totals = [open_sum(f"total{i}", 4 + i, size, i) for i in range(BLOCKS)]
         for t in range(TILES):
             nc.scalar.activation(b[t][:].indirect(n3_list[:]), ra[t // 2][:, W * (t % 2) : W * (t % 2 + 1)], ACT.Copy)
 

from contextlib import ExitStack

import concourse.mybir as mybir
from concourse.masks import make_identity

K, T, S, V, H, W = 512, 2048, 512, 256, 512, 192
FLOPS = 2 * K * H * (2 * S + V) + 2 * H * S * V

F32 = mybir.dt.float32
BF16 = mybir.dt.bfloat16
I32 = mybir.dt.int32
U32 = mybir.dt.uint32
U16 = mybir.dt.uint16
U8 = mybir.dt.uint8
FP8X4 = mybir.dt.float8_e4m3fn_x4
ACT = mybir.ActivationFunctionType
ALU = mybir.AluOpType

P = 128
PACK = 4
TILES = H // P
BLOCKS = S // P
HALF = 256
BANK = 512
QUADRANT = 32
ENTRIES = 16

FIRST_SQUARE_ON_SCALAR = 2
FIRST_TURN_ON_SCALAR = 1
FIRST_N6_ON_SCALAR = 3

PLAIN = "p (m u e) -> p u m e"
DEALT = "p (u m e) -> p u m e"


def tile_picked_twknormbkminthree_none_p_kernel(
    tc, x_words, x_scales, w1, w2, w3, ga, gb, offs, two, n1, n2, three, n3, n4, n5, n6, n7, out
):
    nc = tc.nc
    with ExitStack() as ctx:
        keep = ctx.enter_context(tc.tile_pool(name="keep", bufs=1))
        psum = ctx.enter_context(tc.psum_pool(name="psum", bufs=1))

        def sb(name, shape, dtype):
            return keep.tile(shape, dtype, name=name, align_bytes=64)

        def bank(name, number):
            return psum.tile([P, BANK], F32, name=name, tag=f"bank{number}")

        def load_list(name, src):
            tile = sb(name, list(src.shape), U16)
            nc.sync.dma_start(tile[:], src)
            return tile

        def load_weight(name, w):
            halves = [sb(f"{name}{h}", [P, PACK, HALF], F32) for h in range(2)]
            for h in range(2):
                nc.sync.dma_start(halves[h][:], w[:, HALF * h : HALF * (h + 1)].rearrange("(p j) c -> p j c", j=PACK))
            return halves

        table_scales = sb("table_scales", [P, T], U8)
        nc.gpsimd.memset(table_scales[:].bitcast(I32), 0)
        three_list = load_list("three_list", three)
        table_words = sb("table_words", [P, T], U32)
        nc.sync.dma_start(table_words[:].bitcast(I32), x_words[0].rearrange("p n t -> p (n t)").bitcast(I32))
        two_list = load_list("two_list", two)
        for q in range(P // QUADRANT):
            nc.sync.dma_start(
                table_scales[QUADRANT * q : QUADRANT * q + 4, :].bitcast(I32), x_scales[0, 4 * q : 4 * q + 4, :].bitcast(I32)
            )
        w3_raw = load_weight("w3_raw", w3)
        w2_raw = load_weight("w2_raw", w2)
        n4_list = load_list("n4_list", n4)
        n3_list = load_list("n3_list", n3)
        offs_list = load_list("offs_list", offs)
        w1_raw = load_weight("w1_raw", w1)
        n2_list = load_list("n2_list", n2)
        ga_cols = sb("ga_cols", [P, TILES], F32)
        with nc.allow_non_contiguous_dma(reason="one value of ga for each partition and tile"):
            nc.sync.dma_start(ga_cols[:], ga.rearrange("(t p) o -> p (t o)", p=P))
        n1_list = load_list("n1_list", n1)
        gb_cols = sb("gb_cols", [P, TILES], F32)
        nc.sync.dma_start(gb_cols[:], gb.rearrange("(p t) o -> p (t o)", t=TILES))
        n5_list = load_list("n5_list", n5)
        n6_list = load_list("n6_list", n6)
        n7_list = load_list("n7_list", n7)
        ident = sb("ident", [P, P], F32)
        make_identity(nc, ident[:])

        warm = sb("warm", [P, 2], F32)
        nc.gpsimd.memset(warm[:, 0:1], 1.0)
        nc.scalar.activation(warm[:, 1:2], warm[:, 0:1], ACT.Abs_reciprocal_sqrt)

        def pick(name, entries, n):
            words = sb(name + "_words", [P, n], U32)
            nc.vector.tensor_copy(words[:], table_words[:].indirect(entries[:]))
            scales = sb(name + "_scales", [P, n], U8)
            nc.vector.tensor_copy(scales[:], table_scales[:].indirect(entries[:]))
            return words, scales

        def quantize(name, grouped, n):
            codes = sb(name + "_codes", [P, n], U32)
            scales = sb(name + "_planes", [P, n], U8)
            nc.vector.quantize_mx(out=codes[:].bitcast(FP8X4), scales=scales[:], in_=grouped)
            return codes, scales

        def side_by_side(copy, name, rows):
            grouped = sb(name, [P, HALF * PACK], BF16)
            copy(grouped[:].rearrange("p (c i j) -> p c j i", i=4, j=PACK), rows.rearrange("p j (c i) -> p c j i", i=4))
            return grouped

        def product(dst, stationary, first, moving):
            nc.tensor.matmul_mx(
                out=dst,
                lhsT=stationary[0][:, first : first + P].bitcast(FP8X4),
                lhsT_scale=stationary[1][:, first : first + P],
                rhs=moving[0][:].bitcast(FP8X4),
                rhs_scale=moving[1][:],
                start=True,
                stop=True,
            )

        def look_scalar(dst, window, entries, scale=1.0):
            nc.scalar.activation(dst, window[:].indirect(entries), ACT.Copy, scale=scale)

        def look_vector(dst, window, entries):
            nc.vector.tensor_copy(dst, window[:].indirect(entries))

        def half_of(entries, h):
            return entries[:, HALF // ENTRIES * h : HALF // ENTRIES * (h + 1)]

        def open_sum(name, number, plain, i):
            dst = bank(name, number)
            for t in range(TILES):
                nc.tensor.matmul(
                    dst[:, P * t : P * (t + 1)], plain[t][:, P * i : P * (i + 1)], ident[:], start=t == 0, stop=False, is_transpose=True
                )
            return dst

        def close_sum(dst, looked, i):
            for t in range(TILES):
                nc.tensor.matmul(
                    dst[:, P * t : P * (t + 1)],
                    looked[t][:, P * (i % 2) : P * (i % 2 + 1)],
                    ident[:],
                    start=False,
                    stop=t == TILES - 1,
                    is_transpose=True,
                )


        x_three = pick("x_three", three_list, V)
        w3_grouped = sb("w3_grouped", [P, TILES, P, PACK], BF16)
        for h in range(2):
            nc.scalar.copy(
                w3_grouped[:, :, P // 2 * h : P // 2 * (h + 1), :].rearrange("p t m j -> p m j t"),
                w3_raw[h][:].rearrange("p j (m t) -> p m j t", t=TILES),
            )
        w3_mx = [
            quantize(f"w3_{pair}", w3_grouped[:, 2 * pair : 2 * pair + 2].rearrange("p t m j -> p (t m j)"), HALF) for pair in range(2)
        ]
        x_two = pick("x_two", two_list, S)
        w2_grouped = [
            side_by_side(copy, f"w2_grouped{h}", w2_raw[h][:]) for h, copy in enumerate((nc.scalar.copy, nc.vector.tensor_copy))
        ]
        w2_mx = [quantize(f"w2_{h}", w2_grouped[h][:], HALF) for h in range(2)]

        b = [sb(f"b{t}", [P, V], F32) for t in range(TILES)]
        for pair, copy in enumerate((nc.scalar.copy, nc.vector.tensor_copy)):
            acc = bank(f"b_acc{pair}", 4 + pair)
            for e in range(2):
                product(acc[:, V * e : V * (e + 1)], w3_mx[pair], P * e, x_three)
            for e in range(2):
                copy(b[2 * pair + e][:], acc[:, V * e : V * (e + 1)])

        size = [sb(f"size{t}", [P, S], F32) for t in range(TILES)]
        for t in range(TILES):
            acc = bank(f"d_acc{t}", t)
            product(acc[:], w2_mx[t // 2], P * (t % 2), x_two)
            nc.scalar.activation(size[t][:], acc[:], ACT.Abs)
        totals = [open_sum(f"total{i}", 4 + i, size, i) for i in range(BLOCKS)]

        ra = []
        for pair in range(2):
            pa, old, least = [sb(f"{name}{pair}", [P, 2 * W], F32) for name in ("pa", "old", "least")]
            ra.append(sb(f"ra{pair}", [P, 2 * W], F32))
            for e in range(2):
                look_scalar(pa[:, W * e : W * (e + 1)], b[2 * pair + e], n4_list[:])
                look_scalar(old[:, W * e : W * (e + 1)], b[2 * pair + e], n3_list[:])
            nc.vector.tensor_tensor(least[:], pa[:], old[:], ALU.min)
            nc.vector.scalar_tensor_tensor(ra[pair][:], pa[:], -0.5, least[:], ALU.mult, ALU.add)
        for t in range(TILES):
            nc.scalar.activation(b[t][:].indirect(n3_list[:]), ra[t // 2][:, W * (t % 2) : W * (t % 2 + 1)], ACT.Copy)

        x_offs = pick("x_offs", offs_list, S)
        w1_grouped = [side_by_side(nc.vector.tensor_copy, f"w1_grouped{h}", w1_raw[h][:]) for h in range(2)]
        w1_mx = [quantize(f"w1_{h}", w1_grouped[h][:], HALF) for h in range(2)]
        y = [sb(f"y{t}", [P, S], F32) for t in range(TILES)]
        for t in range(TILES):
            acc = bank(f"y_acc{t}", t)
            product(acc[:], w1_mx[t // 2], P * (t % 2), x_offs)
            nc.vector.tensor_scalar(y[t][:], acc[:], ga_cols[:, t : t + 1], None, ALU.mult)
        diffs = [open_sum(f"diff{i}", i, y, i) for i in range(BLOCKS)]

        y_at = [sb(f"y_at{t}", [P, HALF], F32) for t in range(TILES)]
        size_first = sb("size_first", [P, TILES, HALF], F32)
        size_at = [
            [size_first[:, t, :] for t in range(TILES)],
            [sb(f"size_second{t}", [P, HALF], F32)[:] for t in range(TILES)],
        ]

        def look_up_half(h):
            for t in range(TILES):
                look_scalar(y_at[t][:], y[t], half_of(n1_list, h), scale=-1.0)
                look_vector(size_at[h][t], size[t], half_of(n2_list, h))
            for i in (2 * h, 2 * h + 1):
                close_sum(totals[i], size_at[h], i)

        look_up_half(0)

        z2_rows = size_first[:].bitcast(BF16)[:, :, 0:V]
        for t in range(TILES):
            nc.vector.tensor_scalar(z2_rows[:, t, :], b[t][:], gb_cols[:, t : t + 1], None, ALU.mult)
        z2_mx = quantize("z2", side_by_side(nc.vector.tensor_copy, "z2_grouped", z2_rows)[:], V)

        root = [sb(f"root{i}", [P, H], F32) for i in range(BLOCKS)]

        def z_words(i):
            close_sum(diffs[i], y_at, i)
            diff = diffs[i][:].rearrange(PLAIN, u=2, e=2)
            between = sb(f"between{i}", [P, H], F32)
            z = sb(f"z{i}", [P, H], BF16)
            if i >= FIRST_SQUARE_ON_SCALAR:
                nc.scalar.activation(between[:], root[i][:], ACT.Square)
                nc.vector.tensor_tensor(z[:].rearrange(DEALT, u=2, e=2), diff, between[:].rearrange(DEALT, u=2, e=2), ALU.mult)
            else:
                nc.vector.tensor_tensor(between[:].rearrange(DEALT, u=2, e=2), diff, root[i][:].rearrange(DEALT, u=2, e=2), ALU.mult)
                nc.vector.tensor_tensor(z[:], between[:], root[i][:], ALU.mult)
            return z[:].bitcast(F32)

        def z_quantized(i, words):
            turned = bank(f"turned{i}", 4 + i)
            for u in range(2):
                nc.tensor.transpose(turned[:, P * u : P * (u + 1)], words[:, P * u : P * (u + 1)], ident[:])
            grouped = sb(f"z_grouped{i}", [P, P * PACK], BF16)
            copy = nc.scalar.copy if i >= FIRST_TURN_ON_SCALAR else nc.vector.tensor_copy
            copy(
                grouped[:].bitcast(F32).rearrange("p (r u) -> p r u", u=2),
                turned[:, 0 : 2 * P].rearrange("p (u r) -> p r u", u=2),
            )
            return quantize(f"z_{i}", grouped[:], P)

        z_mx = []
        for h in range(2):
            blocks = (2 * h, 2 * h + 1)
            if h == 1:
                look_up_half(1)
            for i in blocks:
                nc.scalar.activation(
                    root[i][:].rearrange(DEALT, u=2, e=2),
                    totals[i][:].rearrange(PLAIN, u=2, e=2),
                    ACT.Abs_reciprocal_sqrt,
                    bias=0.5,
                )
            words = [z_words(i) for i in blocks]
            z_mx.extend(z_quantized(i, words[i % 2]) for i in blocks)

        s, st, su = size, y, root
        s_at, st_at, su_at, result = [
            [sb(f"{name}{i}", [P, V], F32) for i in range(BLOCKS)] for name in ("s_at", "st_at", "su_at", "result")
        ]
        for i in range(BLOCKS):
            acc = bank(f"s_acc{i}", i)
            product(acc[:, 0:V], z_mx[i], 0, z2_mx)
            nc.scalar.activation(s[i][:, 0:V], acc[:, 0:V], ACT.Copy, scale=0.0625)
        for i in range(BLOCKS):
            look_scalar(s_at[i][:], s[i], n5_list[:])
            nc.vector.tensor_tensor(st[i][:, 0:V], s[i][:, 0:V], s_at[i][:], ALU.subtract)
        for i in range(BLOCKS):
            look = look_scalar if i >= FIRST_N6_ON_SCALAR else look_vector
            look(st_at[i][:], st[i], n6_list[:])
            nc.vector.tensor_tensor(su[i][:, 0:V], st[i][:, 0:V], st_at[i][:], ALU.max)
        for i in range(BLOCKS):
            look_scalar(su_at[i][:], su[i], n7_list[:], scale=0.5)
            nc.vector.tensor_tensor(result[i][:], su[i][:, 0:V], su_at[i][:], ALU.add)
            nc.sync.dma_start(out[P * i : P * (i + 1), :], result[i][:])
